import numpy as np, ml_dtypes
CORES = [36,164,52,180,100,228,116,244]
N = 8
import mx_ref
BF = ml_dtypes.bfloat16
def gcols(t, e):
    v = np.concatenate([t.reshape(8, 16, -1, 4), np.zeros((8, 16, 1, 4), BF)], axis=2)
    return np.ascontiguousarray(np.stack([v[g][:, e[g]] for g in range(8)])).reshape(128, -1)
def tile(rs):
    return np.stack(rs, axis=2).reshape(128, -1).astype(BF)
def cut(t, i, w=512):
    return t[:, w * i:w * i + w]
def pick(q, e):
    c = np.concatenate([q[0].reshape(128, -1, 4), np.zeros((128, 1, 4), np.uint8)], axis=1); s = np.concatenate([q[1], np.ones((16, 1), np.uint8)], axis=1)
    return (np.ascontiguousarray(c[:, e].reshape(128, -1)), np.ascontiguousarray(s[:, e]))
def join(*qs):
    return (np.concatenate([q[0] for q in qs], axis=1), np.concatenate([q[1] for q in qs], axis=1))
def put(q, e, v):
    c, s = q[0].reshape(128, -1, 4).copy(), q[1].copy(); c[:, e] = v[0].reshape(128, -1, 4); s[:, e] = v[1]
    return (c.reshape(128, -1), s)
def pk(c, s):
    return (np.ascontiguousarray(c), mx_ref.live(s))
def emit(q):
    return q[0], q[1]
def packed(v, rng):
    q = [mx_ref.quantize(np.ascontiguousarray(v[r])) for r in range(N)]
    return np.stack([a for a, b in q]), np.stack([mx_ref.plane(b, rng) for a, b in q])
def values_of_codes():
    e, c = np.zeros((128, 128, 4), np.float32), np.zeros((128, 2, 4), np.uint8)
    e[np.arange(128), np.arange(128), 0] = 1
    c[:127, :, 0] = np.arange(256).reshape(2, 128).T[:127]
    return mx_ref.matmul(mx_ref.quantize(e.reshape(128, 512).astype(BF)), (c.reshape(128, 8), np.full((16, 2), 127, np.uint8))).T.reshape(-1).astype(np.float64)
CODE_VALUE, SCALE_VALUE = values_of_codes(), 2.0 ** (np.arange(256) - 127.0)
def decode(q):
    return (CODE_VALUE[q[0]].reshape(16, 8, -1, 4) * SCALE_VALUE[q[1]][:, None, :, None] + 0.0).reshape(128, -1).astype(np.float32)
def f(rng, *shape):
    return mx_ref.flush((rng.standard_normal(shape, dtype=np.float32) * np.exp2(rng.integers(-2, 3, shape[:-1] + (1,)))).astype(BF))
def wide(rng, *shape, cols=0):
    v = rng.standard_normal(shape, dtype=np.float32) * np.exp2(rng.integers(-12, 13, shape)).astype(np.float32)
    if cols: v *= np.repeat(np.exp2(rng.integers(-cols, cols + 1, shape[:-2] + (1, shape[-1] // 4))) * (rng.random(shape[:-2] + (1, shape[-1] // 4)) > 0.0625), 4, axis=-1).astype(np.float32)
    return mx_ref.flush(v.astype(BF))
C, H, R, STEP = 288, 128, 3, 9
def big(v):
    v = v.astype(np.float32)
    v[np.abs(v) < np.float32(2.0 ** -16)] = 0
    return v.astype(BF)
def numbers_of(rng):
    return {"x": big(f(rng, N, 128, 4 * C)), "u": np.array(f(rng, N, 128, 512)), "v": np.array(f(rng, N, 128, 512))}
def plays(rng):
    return rng.integers(1, 7, (N, 8, 1)).astype(np.int32)
def layers(rng):
    return big(f(rng, N, 128, 2048)).reshape(N, 8, 16, 4, 8, 16, 4)
def weights(rng, w):
    c, s = packed(np.ascontiguousarray(w).reshape(N, 128, 2048), rng)
    return {"wc": c, "ws": s}
def turning(rng):
    b = np.abs(128 - (STEP * np.arange(130)) % 256)
    k = np.flatnonzero((b[1:129] - b[:128]) * (b[2:] - b[1:129]) < 0) + 1
    e = min(STEP, C // 32) - 1
    k = np.concatenate([[0], k[:e], [128]])
    s = -np.ones(C)
    for i in range(e + 1):
        lo = 32 * i
        hi = lo + 32 if i < e else C
        m = [lo, hi - 1]
        w = rng.permutation(np.setdiff1d(np.arange(lo, hi), m))
        s[m] = 1
        s[w[:k[i + 1] - k[i] - len(m)]] = 1
    return s
def setup_inputs(rng):
    return {**numbers_of(rng), "p": plays(rng), **weights(rng, layers(rng))}
def setup_inputs_ties(rng):
    d = numbers_of(rng)
    e = rng.permutation(N)
    x = d["x"].reshape(N, 8, 16, C, 4)
    a = (1.0 + (2 * rng.integers(0, 64, (N, 8, 8, C, 4)) + 1) * 2.0 ** -7) * np.exp2(-rng.integers(8, 15, (N, 8, 8, C, 4)).astype(np.float64))
    a *= rng.integers(0, 2, a.shape) * 2.0 - 1.0
    a[:, :, 0, :, 0] = 1.96875
    x[:, :, 8:] = a.astype(np.float32).astype(BF)
    for r in range(N):
        k = rng.permutation(C) % 3
        if r == e[0]: k = np.ones(C, int)
        elif r in e[2::2]: k = rng.permutation(3)[np.arange(C) % 3]
        c = x[r, 0, :8, :3].copy()
        c[:, 0] = 0
        c[:, 2] = -c[:, 1]
        x[r, 0, :8] = c[:, k]
    x[e[1]] = 0
    u = d["u"].reshape(N, 8, 16, 128, 4)
    u[:, 1:, :, 0] = 0
    u[:, 0, 8:, 0] = 0
    w = layers(rng)
    w[:, :, :, :, 0, :8] = 0
    return {"x": x.reshape(N, 128, 4 * C), "u": u.reshape(N, 128, 512), "v": d["v"], "p": plays(rng), **weights(rng, w)}
def setup_inputs_near(rng):
    d = numbers_of(rng)
    x = d["x"].reshape(N, 8, 16, C, 4)
    u = d["u"].reshape(N, 128, 128, 4)
    o = rng.permutation(N) % 2
    x[:, 0, 0] = 0
    x[:, 0, 8:] = 0
    u[:, :, 0] = 0
    for r in range(N):
        k = 2.0 ** -30 if o[r] == 0 else 1.0
        c = rng.permutation(C) % 3
        x[r, 0, 8, :, 0] = (np.array([9, 8, 9])[c] * 0.125 * k).astype(np.float32).astype(BF)
        x[r, 0, 9, :, 0] = (np.array([10, 9, 11])[c] * 0.125 * k).astype(np.float32).astype(BF)
        x[r, 0, 0, rng.integers(C), 0] = 2.0 ** 29 * (rng.integers(0, 2) * 2.0 - 1.0)
        u[r, 0, 0, 0] = k
        u[r, 8, 0, 0] = 1.125 * k
        u[r, 9, 0, 0] = -k
    w = layers(rng)
    for i in [0] + [8 + j for j in range(8)]:
        w[:, 0, i] = 0
        w[:, :, :, :, 0, i] = 0
    return {"x": x.reshape(N, 128, 4 * C), "u": u.reshape(N, 128, 512), "v": d["v"], "p": plays(rng), **weights(rng, w)}
def setup_inputs_late(rng):
    d = numbers_of(rng)
    x = d["x"].reshape(N, 128, C, 4)
    k = rng.permutation(N) % 2
    c = (k * 2.0 - 1.0).astype(np.float32).astype(BF)
    x[:, 0] = c[:, None, None]
    x[:, 1:8] = np.clip(x[:, 1:8].astype(np.float32), -8, 8).astype(BF)
    u = d["u"].reshape(N, 128, 128, 4)
    u[:, :, 0] = 0
    u[:, 0, 0, 0] = 1
    p = plays(rng)
    p[k == 0, 0] = 1
    p[np.flatnonzero(k == 1)[0]] = 6
    return {"x": x.reshape(N, 128, 4 * C), "u": u.reshape(N, 128, 512), "v": d["v"], "p": p, **weights(rng, layers(rng))}
def setup_inputs_ends(rng):
    d = numbers_of(rng)
    x = np.zeros((N, 8, 16, C, 4), np.float32)
    u = d["u"].reshape(N, 128, 128, 4)
    v = d["v"]
    o = rng.permutation(N) % 4
    for t in range(N):
        for r in range(N):
            if o[r] == 3 and o[(r + 1) % N] == 2:
                o[r] = 2
                o[(r + 1) % N] = 3
    h = rng.permutation(N) % 2
    m = np.flatnonzero(o == 1)
    if (h[m] == 0).all():
        h[np.flatnonzero(h == 1)[0]] = 0
        h[m[0]] = 1
    p = np.zeros((N, 8, 1), np.int32)
    w = np.zeros((N, 128, 4, 128, 4), np.float32)
    i = np.arange(128)
    u[:, :, 0] = 0
    for r in range(N):
        p[r] = 6 if h[r] == 0 else 1
        for b in range(4): w[r, i, b, i, b] = 1 if o[r] == 3 else -1
        if o[r] < 3:
            a = rng.integers(8, 17, (8, 1, C, 1)) * 2.0 ** 26
            x[r] = a if o[r] == 0 else -a if o[r] == 1 else a * turning(rng)[None, None, :, None]
            u[r, :, 0] = 2.0 ** 30
        else:
            x[r] = rng.integers(8, 16, (8, 1, C, 1)) * 2.0 ** -33
            x[r, 0, 0, :, 0] = (2 + rng.permutation(C) % 3) * 2.0 ** -31
            x[r, 0, 1, :, 0] = 2.0 ** -30
            u[r, 0, 0, 0] = 2.0 ** -30
            u[r, 1, 0, 0] = -1.5 * 2.0 ** -30
        if o[r] in (0, 2): v[r] = (2.0 ** 30 * (rng.integers(0, 2, (128, 512)) * 2.0 - 1.0)).astype(np.float32).astype(BF)
        if o[r] == 3: v[r] = 2.0 ** -30
    return {"x": x.reshape(N, 128, 4 * C).astype(BF), "u": u.reshape(N, 128, 512), "v": v, "p": p, **weights(rng, w.astype(BF))}
def setup_inputs_spread(rng):
    d = setup_inputs(rng)
    d["x"] = big(wide(rng, N, 128, 4 * C, cols=6))
    return d
def check_inputs(d):
    b = []
    for k in ("x", "u", "v"):
        a = np.abs(d[k].astype(np.float32))
        if not (np.isfinite(a).all() and ((a == 0) | (a >= 2.0 ** -30) & (a <= 2.0 ** 30)).all()): b.append("a value of " + k)
    if not ((d["p"] >= 1) & (d["p"] <= 6)).all(): b.append("an entry of p")
    none, least, most = [emit(mx_ref.quantize(np.full((128, 16), k, np.float32).astype(BF)))[1][0, 0] for k in (0.0, 2.0 ** -30, 2.0 ** 30)]
    for r in range(N):
        if ((d["wc"][r] == 0x7F) | (d["wc"][r] == 0xFF)).any(): b.append("wc: a code that is no number")
        s = mx_ref.live(d["ws"][r])
        if ((s != none) & ((s < least) | (s > most))).any(): b.append("ws: a scale out of range")
    return b
def reference(x, u, v, p, wc, ws):
    qu = [mx_ref.quantize(u[r]) for r in range(N)]
    lay = [pk(wc[r], ws[r]) for r in range(N)]
    now = [x[r] for r in range(N)]
    n, kept = np.zeros(N, np.int64), np.zeros((N, 8), np.int64)
    a = np.zeros((N, 8, C), np.int64)
    for t in range(R):
        q = [mx_ref.quantize(now[r]) for r in range(N)]
        held = [decode(q[r]).astype(BF) for r in range(N)]
        s = np.stack([mx_ref.matmul(qu[r], q[r])[0] > 0 for r in range(N)])
        for j in range(C):
            n = n + s[:, j]
            c = np.abs(128 - (STEP * n) % 256)
            for g in range(8):
                c = np.minimum(np.maximum(kept[:, g], c - p[:, g, 0]), c + p[:, g, 0])
                kept[:, g] = c
            a[:, :, j] = kept
        made = []
        for r in range(N):
            window = np.concatenate([held[r], cut(held[(r + 1) % N], 0, 4 * H)], axis=1)
            far = gcols(window, np.arange(C) + a[r])
            z = mx_ref.quantize(((held[r].astype(np.float32) + far.astype(np.float32)) * np.float32(0.5)).astype(BF))
            made.append(tile([mx_ref.matmul(pick(lay[r], np.arange(128 * b, 128 * b + 128)), z) * np.float32(0.03125) + now[r][:, b::4].astype(np.float32) for b in range(4)]))
        now = made
    y, ao = np.zeros((N, 128, C), np.float32), np.zeros((N, 8, C), np.float32)
    oc, osc = np.zeros((N, 128, 4 * C), np.uint8), np.zeros((N, 16, C), np.uint8)
    for r in range(N):
        q = mx_ref.quantize(now[r])
        y[r] = mx_ref.matmul(mx_ref.quantize(v[r]), q)
        ao[r] = a[r]
        oc[r], osc[r] = emit(q)
    return {"y": y, "ao": ao, "oc": oc, "osc": osc}

@@ -1,0 +1,378 @@
+from concourse.bass import DstId, RemoteDMATransfer
+from concourse.mybir import dt, AluOpType as O, AxisListType, ActivationFunctionType as F
+
+C, H, R, W = 288, 128, 3, 416
+C0 = (0, 128)
+NB = (128, 160)
+TAB = 880
+
+F8 = "float8_e4m3fn_x4"
+SCRATCH = {
+    "X0": ("sbuf", [128, 4 * C], "bfloat16"), "X1": ("sbuf", [128, 4 * C], "bfloat16"),
+    "X2": ("sbuf", [128, 4 * C], "bfloat16"), "X3": ("sbuf", [128, 4 * C], "bfloat16"),
+    "ut": ("sbuf", [128, 512], "bfloat16"), "vt": ("sbuf", [128, 512], "bfloat16"),
+    "uq": ("sbuf", [128, 128], F8), "us": ("sbuf", [128, 128], "uint8"),
+    "u2q": ("sbuf", [128, 128], F8), "u2s": ("sbuf", [128, 128], "uint8"),
+    "vq": ("sbuf", [128, 128], F8), "vs": ("sbuf", [128, 128], "uint8"),
+    "wq": ("sbuf", [128, 512], F8), "wsc": ("sbuf", [128, 512], "uint8"),
+    "cst": ("sbuf", [128, 128], "bfloat16"),
+    "e0": ("sbuf", [128, 516], "bfloat16"), "e1": ("sbuf", [128, 516], "bfloat16"), "e2": ("sbuf", [128, 516], "bfloat16"),
+    "eq": ("sbuf", [128, 1536], F8), "es": ("sbuf", [128, 1536], "uint8"),
+    "off0": ("sbuf", [128, 8], "uint16"),
+    "pci": ("sbuf", [128, 4], "int32"), "pcf": ("sbuf", [128, 16], "float32"),
+    "di": ("sbuf", [128, 64], "int32"), "df": ("sbuf", [128, 32], "float32"), "hold": ("sbuf", [128, 320], "bfloat16"),
+    "ti": ("sbuf", [128, 512], "int32"), "tf": ("sbuf", [128, 256], "float32"), "tab": ("sbuf", [128, TAB], "bfloat16"),
+    "m16": ("sbuf", [128, 10], "float32"), "base": ("sbuf", [128, 36], "float32"),
+    "one8": ("sbuf", [128, 8], "float32"), "mk": ("sbuf", [128, 16], "float32"),
+    "pin": ("sbuf", [1, 8], "int32"), "pfl": ("sbuf", [1, 8], "float32"), "pbc": ("sbuf", [128, 8], "float32"),
+    "pm": ("sbuf", [128, 16], "float32"),
+    "carry": ("sbuf", [128, 16], "float32"),
+    "pos": ("sbuf", [128, R * C], "bfloat16"), "cnt": ("sbuf", [128, R * C], "bfloat16"),
+    "hn": ("sbuf", [128, R * C], "bfloat16"), "bt": ("sbuf", [128, R * C], "bfloat16"),
+    "nw": ("sbuf", [128, R * 18], "uint16"),
+    "d1": ("sbuf", [128, R * 2 * C], "bfloat16"), "pl": ("sbuf", [128, R * 2 * C], "bfloat16"),
+    "hh": ("sbuf", [128, R * 2 * C], "bfloat16"),
+    "of": ("sbuf", [128, R * 36], "float32"), "off": ("sbuf", [128, R * 36], "uint16"),
+    "zt": ("sbuf", [128, R * 4 * C], "bfloat16"),
+    "zq": ("sbuf", [128, R * C], F8), "zs": ("sbuf", [128, R * C], "uint8"),
+    "ysb": ("sbuf", [128, C], "float32"), "ao0": ("sbuf", [128, C], "float32"), "ao1": ("sbuf", [128, C], "float32"),
+    "ps": ("psum", [128, 4096], "float32"),
+}
+for _t in range(R + 1):
+    SCRATCH["q%d" % _t] = ("sbuf", [128, W], F8)
+    SCRATCH["s%d" % _t] = ("sbuf", [128, W], "uint8")
+for _t in range(R):
+    for _k in range(2):
+        SCRATCH["f%d%d" % (_t, _k)] = ("sbuf", [128, 2 * NB[_k]], F8)
+        SCRATCH["g%d%d" % (_t, _k)] = ("sbuf", [128, 2 * NB[_k]], "uint8")
+SEMAPHORES = ["V", "S", "T", "G", "dXA", "dXB", "dU", "dP", "dW", "dV", "arr0", "arr1", "arr2", "sent", "outA", "outB"]
+
+
+def rank_program(g, core, T, topo):
+    rank = T.rank_of(core)
+    if rank is None:
+        return
+    n_ranks = len(T.cores)
+    prev = T.cores[(rank - 1) % n_ranks]
+    nxt = T.cores[(rank + 1) % n_ranks]
+    eng = {"V": g.vector, "S": g.scalar, "T": g.tensor, "G": g, "Y": g.sync}
+    count = {"V": 0, "S": 0, "T": 0, "G": 0}
+    known = {}
+
+    def need(q, toks):
+        best = {}
+        for tk in toks:
+            if tk is None:
+                continue
+            best[tk[0]] = max(best.get(tk[0], 0), tk[1])
+        for s in best:
+            if best[s] > known.get((q, s), 0):
+                eng[q].wait_ge(T.sem[s], best[s])
+                known[(q, s)] = best[s]
+
+    def run(q, deps, call):
+        need(q, deps)
+        call().then_inc(T.sem[q], 1)
+        count[q] += 1
+        return (q, count[q])
+
+    def ts(out, in0, s1, op0, s2=None, op1=None):
+        if op1 is None:
+            return lambda: g.vector.tensor_scalar(out, in0, s1, None, op0)
+        return lambda: g.vector.tensor_scalar(out, in0, s1, s2, op0, op1)
+
+    def tt(out, a, b, op):
+        return lambda: g.vector.tensor_tensor(out, a, b, op)
+
+    def cp(out, in_):
+        return lambda: g.vector.tensor_copy(out, in_)
+
+    def scan(out, d0, d1, init, op0, op1):
+        return lambda: g.vector.tensor_tensor_scan(out, d0, d1, init, op0, op1)
+
+    def act(out, in_, f=F.Copy, **kw):
+        return lambda: g.scalar.activation(out, in_, f, **kw)
+
+    def quant(q, s, t):
+        return lambda: g.vector.quantize_mx(q, s, t)
+
+    def mm(bank, n, lq, ls, rq, rs, start=True, stop=True):
+        return lambda: g.tensor.matmul_mx(T.ps[:, 512 * bank:512 * bank + n], lq, ls, rq, rs, start, stop)
+
+    g.sync.dma_start(T.X0[:, 0:512], T.x[:, 0:512]).then_inc(T.sem.dXA, 16)
+    g.scalar.dma_start(T.ut[:, :], T.u[:, :]).then_inc(T.sem.dU, 16)
+    g.scalar.dma_start(T.pin[0:1, :], T.p[:, :]).then_inc(T.sem.dP, 16)
+    g.sync.dma_start(T.X0[:, 512:1152], T.x[:, 512:1152]).then_inc(T.sem.dXB, 16)
+    g.sync.dma_start(T.wq[:, :].bitcast(dt.uint8), T.wc[:, :]).then_inc(T.sem.dW, 16)
+    g.sync.dma_start(T.wsc[:, :], T.ws[:, :]).then_inc(T.sem.dW, 16)
+    g.sync.dma_start(T.vt[:, :], T.v[:, :]).then_inc(T.sem.dV, 16)
+
+    c_cst = run("V", [], lambda: g.vector.memset(T.cst[:, :], 2.0 ** -6))
+    c_e0 = run("V", [], lambda: g.vector.memset(T.e0[:, :], 0.0))
+    c_off0 = run("V", [], lambda: g.vector.memset(T.off0[:, :], 0))
+    c_one = run("V", [], lambda: g.vector.memset(T.one8[:, :], 1.0))
+    i_p = run("G", [], lambda: g.iota(T.pci[:, 0:1], [[0, 1]], 0, 1))
+    i_d = run("G", [], lambda: g.iota(T.di[:, 0:32], [[1, 32]], 128, -1))
+    a_e0 = run("G", [c_cst, c_e0], lambda: g.affine_select(T.e0[:, 3:515:4], T.cst[:, :], [[-1, 128]], O.is_equal, 0.0, 0, 1))
+    i_t = run("G", [], lambda: g.iota(T.ti[:, 0:256], [[9, 256]], 0, 0))
+    i_m = run("G", [], lambda: g.iota(T.m16[:, :], [[16, 10]], 0, 0, allow_small_or_imprecise_dtypes=True))
+    a_m0 = run("G", [c_one], lambda: g.affine_select(T.mk[:, 0:8], T.one8[:, :], [[-32, 4], [-32, 2]], O.is_ge, 0.0, 0, 1))
+    a_m1 = run("G", [c_one], lambda: g.affine_select(T.mk[:, 8:16], T.one8[:, :], [[-32, 4], [0, 2]], O.is_ge, 0.0, 0, 1))
+
+    col = lambda k: T.pcf[:, k:k + 1]
+    h = run("V", [i_p], ts(T.pci[:, 1:2], T.pci[:, 0:1], 16, O.bitwise_and))
+    q15 = run("V", [i_p], ts(T.pci[:, 2:3], T.pci[:, 0:1], 15, O.bitwise_and))
+    d_and = run("V", [i_d], ts(T.di[:, 32:64], T.di[:, 0:32], 15, O.bitwise_and))
+    k_e = run("V", [h], ts(col(0), T.pci[:, 1:2], 0.0, O.is_equal))
+    k_o = run("V", [h], ts(col(1), T.pci[:, 1:2], 0.0, O.is_gt))
+    k_q = run("V", [q15], ts(col(2), T.pci[:, 2:3], -9.0, O.mult, 150.0, O.add))
+    carry = [run("V", [q15], ts(T.carry[:, 0:1], T.pci[:, 2:3], -10.0, O.mult, 150.0, O.add)), 0]
+    d_f = run("V", [d_and], ts(T.df[:, :], T.di[:, 32:64], 0.0, O.is_gt, -522.0, O.mult))
+    t_and = run("V", [i_t], ts(T.ti[:, 256:512], T.ti[:, 0:256], 255, O.bitwise_and))
+    d_h = run("V", [d_f], ts(T.hold[:, 0:32], T.df[:, :], 512.0, O.add))
+    t_f = run("V", [t_and], ts(T.tf[:, :], T.ti[:, 256:512], -128.0, O.add))
+    d_h = run("V", [d_h], cp(T.hold[:, 32:64], T.hold[:, 0:32]))
+    d_h = run("V", [d_h], cp(T.hold[:, 64:128], T.hold[:, 0:64]))
+    d_h = run("V", [d_h], cp(T.hold[:, 128:256], T.hold[:, 0:128]))
+    d_h = run("V", [d_h], cp(T.hold[:, 256:320], T.hold[:, 0:64]))
+    m_t = [run("S", [t_f], act(T.tab[:, 0:256], T.tf[:, :], F.Abs)), None, None, None]
+    m_e = [a_e0,
+           run("S", [a_e0, k_e], act(T.e1[:, :], T.e0[:, :], F.Copy, scale=col(0))),
+           run("S", [a_e0, k_o], act(T.e2[:, :], T.e0[:, :], F.Copy, scale=col(1)))]
+    E = {}
+
+    def equant(y, b):
+        k = 128 * (4 * y + b)
+        src = (T.e0, T.e1, T.e2)[y]
+        E[y, b] = run("V", [m_e[y]], quant(T.eq[:, k:k + 128], T.es[:, k:k + 128], src[:, 3 - b:515 - b]))
+
+    def eside(y, b):
+        k = 128 * (4 * y + b)
+        return T.eq[:, k:k + 128], T.es[:, k:k + 128]
+
+    uq = run("V", [("dU", 16)], quant(T.uq[:, :], T.us[:, :], T.ut[:, :]))
+    u2 = [run("V", [uq, c_off0], cp(T.u2q[:, 0:128].bitcast(dt.uint32), T.uq[:, 0:128].bitcast(dt.uint32).indirect(T.off0[:, 0:8]))),
+          run("S", [uq, c_off0], act(T.u2s[:, 0:128], T.us[:, 0:128].indirect(T.off0[:, 0:8])))]
+
+    QT = [T.q0, T.q1, T.q2, T.q3]
+    ST = [T.s0, T.s1, T.s2, T.s3]
+    XT = [T.X0, T.X1, T.X2, T.X3]
+    bank = {}
+    qx, S, st = {}, {}, {}
+
+    def sl(k):
+        return slice(C0[k], C0[k] + NB[k])
+
+    def quantx(t, k, deps):
+        a, n = C0[k], NB[k]
+        qx[t, k] = run("V", deps, quant(QT[t][:, a:a + n], ST[t][:, a:a + n], XT[t][:, 4 * a:4 * a + 4 * n]))
+
+    def send(t):
+        need("G", [qx[t, 0]])
+        rid, pid = topo.addr(prev, core)
+        m = topo.mask(core, prev)
+        g.remote_dma(QT[t][:, C:W].bitcast(dt.uint8), QT[t][:, 0:H].bitcast(dt.uint8), T.sem["arr%d" % t], T.sem.sent, pid, rid, m)
+        g.remote_dma(ST[t][:, C:W], ST[t][:, 0:H], T.sem["arr%d" % t], T.sem.sent, pid, rid, m)
+
+    def sprod(t, k):
+        bk = 4 * k + 3
+        S[t, k] = run("T", [qx[t, k], bank.get(bk)] + u2,
+                      mm(bk, NB[k], T.u2q[:, :], T.u2s[:, :], QT[t][:, sl(k)], ST[t][:, sl(k)]))
+
+    def chain1(t, k):
+        n, a = NB[k], C * t + C0[k]
+        bk = 4 * k + 3
+        x = run("V", [S[t, k]], ts(T.pos[:, a:a + n], T.ps[:, 512 * bk:512 * bk + n], 0.0, O.is_gt))
+        bank[bk] = x
+        x = run("V", [x], scan(T.cnt[:, a:a + n], T.pos[:, a:a + n], T.pos[:, a:a + n], 0.0, O.add, O.max))
+        y = run("V", [x, d_h], scan(T.hn[:, a:a + n], T.hold[:, 0:n], T.cnt[:, a:a + n], 0.0, O.add, O.min))
+        w = 18 * t + 8 * k
+        cc = carry[1]
+        st[t, k, "nw"] = run("V", [y, carry[0]], ts(T.nw[:, w:w + n // 16], T.hn[:, a + 15:a + n:16], T.carry[:, cc:cc + 1], O.add))
+        carry[0] = run("V", [x, carry[0]], tt(T.carry[:, cc + 1:cc + 2], T.carry[:, cc:cc + 1], T.cnt[:, a + n - 1:a + n], O.add))
+        carry[1] = cc + 1
+
+    def gath(t, k):
+        n, a, w = NB[k], C * t + C0[k], 18 * t + 8 * k
+        width = (256, 512)[k] if t == 0 else TAB
+        st[t, k, "b"] = run("S", [st[t, k, "nw"]] + m_t[:1 if width == 256 else 2 if width == 512 else 4],
+                            act(T.bt[:, a:a + n], T.tab[:, 0:width].indirect(T.nw[:, w:w + n // 16])))
+
+    last = {}
+
+    def chain2a(t, k):
+        n, a, d = NB[k], C * t + C0[k], 2 * (C * t + C0[k])
+        x = [run("V", [st[t, k, "b"], sc[l]], ts(T.d1[:, d + l * n:d + l * n + n], T.bt[:, a:a + n], col(3 + l), O.add, col(3 + l), O.add)) for l in range(2)]
+        pp = []
+        for l in range(2):
+            init, tok = last.get(l, (col(3 + l), None))
+            e = d + l * n
+            pt = run("V", [x[l], st[t, k, "b"], tok], scan(T.pl[:, e:e + n], T.bt[:, a:a + n], T.d1[:, e:e + n], init, O.max, O.min))
+            last[l] = (T.pl[:, e + n - 1:e + n], pt)
+            pp.append(pt)
+        st[t, k, "pl"] = pp
+
+    def chain2b(t, k):
+        n, d, o = NB[k], 2 * (C * t + C0[k]), 36 * t + 16 * k
+        m = 2 * n // 16
+        x = run("V", st[t, k, "pl"] + [d_h], scan(T.hh[:, d:d + 2 * n], T.hold[:, 0:2 * n], T.pl[:, d:d + 2 * n], 0.0, O.add, O.min))
+        x = run("V", [x] + bs, tt(T.of[:, o:o + m], T.hh[:, d + 15:d + 2 * n:16], T.base[:, 16 * k:16 * k + m], O.add))
+        st[t, k, "off"] = run("V", [x], cp(T.off[:, o:o + m], T.of[:, o:o + m]))
+
+    def picks(t, k):
+        n, o = NB[k], 36 * t + 16 * k
+        lo, hi = (0, C) if k == 0 else (H, W)
+        fq, fs = T["f%d%d" % (t, k)], T["g%d%d" % (t, k)]
+        deps = [st[t, k, "off"], qx[t, 0], qx[t, 1]] + ([("arr%d" % t, 2 * len(topo.engines(nxt, core)))] if k else [])
+        for l in range(2):
+            off = T.off[:, o + l * n // 16:o + (l + 1) * n // 16]
+            c, d = l * n, (l + 1) * n
+            st[t, k, "pk", l] = [
+                run("V", deps, cp(fq[:, c:d].bitcast(dt.uint32), QT[t][:, lo:hi].bitcast(dt.uint32).indirect(off))),
+                run("S", deps, act(fs[:, c:d], ST[t][:, lo:hi].indirect(off)))]
+
+    def own(t, k):
+        for b in range(4):
+            bk = 4 * k + b
+            lq, ls = eside(0, b)
+            run("T", [E[0, b], qx[t, k], bank.get(bk)], mm(bk, NB[k], lq, ls, QT[t][:, sl(k)], ST[t][:, sl(k)], True, False))
+
+    def far(t, k, l):
+        n = NB[k]
+        fq, fs = T["f%d%d" % (t, k)], T["g%d%d" % (t, k)]
+        for b in range(4):
+            lq, ls = eside(1 + l, b)
+            st[t, k, "z", b] = run("T", [E[1 + l, b]] + st[t, k, "pk", l],
+                                   mm(4 * k + b, n, lq, ls, fq[:, l * n:l * n + n], fs[:, l * n:l * n + n], False, l == 1))
+
+    def cast(t, k, b):
+        n, z = NB[k], 4 * (C * t + C0[k])
+        st[t, k, "c", b] = bank[4 * k + b] = run("S", [st[t, k, "z", b]], act(T.zt[:, z + b:z + 4 * n:4], T.ps[:, 512 * (4 * k + b):512 * (4 * k + b) + n]))
+
+    def qz(t, k):
+        n, a = NB[k], C * t + C0[k]
+        st[t, k, "qz"] = run("V", [st[t, k, "c", b] for b in range(4)], quant(T.zq[:, a:a + n], T.zs[:, a:a + n], T.zt[:, 4 * a:4 * a + 4 * n]))
+
+    def wprod(t, k):
+        n, a = NB[k], C * t + C0[k]
+        for b in range(4):
+            st[t, k, "r", b] = run("T", [("dW", 32), st[t, k, "qz"], bank.get(4 * k + b)],
+                                   mm(4 * k + b, n, T.wq[:, 128 * b:128 * b + 128], T.wsc[:, 128 * b:128 * b + 128], T.zq[:, a:a + n], T.zs[:, a:a + n]))
+
+    def xupd(t, k, bs_):
+        n, a, e = NB[k], 4 * C0[k], 4 * (C0[k] + NB[k])
+        for b in bs_:
+            st[t, k, "x", b] = bank[4 * k + b] = run(
+                "V", [st[t, k, "r", b], ("dXA", 16) if t == 0 and k == 0 else ("dXB", 16) if t == 0 else st[t - 1, k, "x", b]],
+                tt(XT[t + 1][:, a + b:e:4], T.ps[:, 512 * (4 * k + b):512 * (4 * k + b) + n], XT[t][:, a + b:e:4], O.add))
+
+    def newx(t, k):
+        quantx(t + 1, k, [st[t, k, "x", b] for b in range(4)])
+
+    def yprod(k):
+        n = NB[k]
+        bk = 4 * k
+        x = run("T", [vq, qx[R, k], bank.get(bk)], mm(bk, n, T.vq[:, :], T.vs[:, :], T.q3[:, sl(k)], T.s3[:, sl(k)]))
+        return run("S", [x], act(T.ysb[:, sl(k)], T.ps[:, 512 * bk:512 * bk + n]))
+
+    quantx(0, 0, [("dXA", 16)])
+    pf = run("V", [("dP", 16)], cp(T.pfl[0:1, :], T.pin[0:1, :]))
+    send(0)
+    pb = run("G", [pf], lambda: g.partition_broadcast(T.pbc[:, :], T.pfl[0:1, :], 128))
+    sprod(0, 0)
+    equant(0, 0)
+    equant(0, 1)
+    chain1(0, 0)
+    gath(0, 0)
+    m_t[1] = run("V", [m_t[0]], cp(T.tab[:, 256:512], T.tab[:, 0:256]))
+    pm = [run("V", [pb, (a_m0, a_m1)[l]], tt(T.pm[:, 8 * l:8 * l + 8], T.pbc[:, :], T.mk[:, 8 * l:8 * l + 8], O.mult)) for l in range(2)]
+    sc = [run("V", [pm[l]], lambda l=l: g.vector.tensor_reduce(col(3 + l), T.pm[:, 8 * l:8 * l + 8], AxisListType.X, O.add)) for l in range(2)]
+    ns = [run("V", [sc[l]], ts(col(5 + l), col(3 + l), -1.0, O.mult)) for l in range(2)]
+    cc2 = [run("V", [sc[l], k_q], tt(col(7 + l), col(2), col(3 + l), O.subtract)) for l in range(2)]
+    bs = []
+    for l in range(2):
+        bs.append(run("V", [cc2[l], i_m], ts(T.base[:, 8 * l:8 * l + 8], T.m16[:, 0:8], col(7 + l), O.add)))
+        bs.append(run("V", [cc2[l], i_m], ts(T.base[:, 16 + 10 * l:26 + 10 * l], T.m16[:, 0:10], col(7 + l), O.add)))
+    quantx(0, 1, [("dXB", 16)])
+    equant(0, 2)
+    equant(0, 3)
+    chain2a(0, 0)
+    for b in range(4):
+        equant(1, b)
+    chain2b(0, 0)
+    own(0, 0)
+    m_t[2] = run("S", [m_t[0]], act(T.tab[:, 512:768], T.tab[:, 0:256]))
+    m_t[3] = run("S", [m_t[0]], act(T.tab[:, 768:880], T.tab[:, 0:112]))
+    vq = None
+
+    for t in range(R):
+        sprod(t, 1)
+        picks(t, 0)
+        if t == 0:
+            for b in range(4):
+                equant(2, b)
+        far(t, 0, 0)
+        far(t, 0, 1)
+        chain1(t, 1)
+        cast(t, 0, 0)
+        gath(t, 1)
+        for b in range(1, 4):
+            cast(t, 0, b)
+        chain2a(t, 1)
+        qz(t, 0)
+        chain2b(t, 1)
+        own(t, 1)
+        wprod(t, 0)
+        picks(t, 1)
+        far(t, 1, 0)
+        far(t, 1, 1)
+        xupd(t, 0, range(4))
+        newx(t, 0)
+        if t < R - 1:
+            send(t + 1)
+        for b in range(4):
+            cast(t, 1, b)
+        if t < R - 1:
+            sprod(t + 1, 0)
+        qz(t, 1)
+        wprod(t, 1)
+        if t < R - 1:
+            chain1(t + 1, 0)
+            gath(t + 1, 0)
+            if t == 0:
+                vq = run("V", [("dV", 16)], quant(T.vq[:, :], T.vs[:, :], T.vt[:, :]))
+            xupd(t, 1, range(2))
+            chain2a(t + 1, 0)
+            xupd(t, 1, range(2, 4))
+            chain2b(t + 1, 0)
+            newx(t, 1)
+            own(t + 1, 0)
+        else:
+            y0 = yprod(0)
+            need("Y", [qx[R, 0]])
+            g.sync.dma_start(T.oc[:, 0:512], T.q3[:, 0:128].bitcast(dt.uint8)).then_inc(T.sem.outA, 16)
+            need("Y", [y0])
+            g.sync.dma_start(T.y[:, 0:128], T.ysb[:, 0:128]).then_inc(T.sem.outA, 16)
+            ax = []
+            for kk in range(2):
+                n, d = NB[kk], 2 * (C * t + C0[kk])
+                for l in range(2):
+                    ax.append(run("S", st[t, kk, "pl"] + [ns[l]], act((T.ao0, T.ao1)[l][:, sl(kk)], T.pl[:, d + l * n:d + l * n + n], F.Identity, bias=col(5 + l))))
+            need("Y", ax)
+            for l in range(2):
+                g.sync.dma_start(T.ao[l:8:2, :], (T.ao0, T.ao1)[l][0:128:32, :]).then_inc(T.sem.outA, 16)
+            xupd(t, 1, range(4))
+            newx(t, 1)
+    y1 = yprod(1)
+    need("Y", [qx[R, 1]])
+    for k in range(3):
+        g.sync.dma_start(T.osc[4 * k:4 * k + 4, :], T.s3[32 * k:32 * k + 4, 0:C]).then_inc(T.sem.outA, 16)
+    g.scalar.dma_start(T.oc[:, 512:1152], T.q3[:, 128:288].bitcast(dt.uint8)).then_inc(T.sem.outB, 16)
+    g.scalar.dma_start(T.osc[12:16, :], T.s3[96:100, 0:C]).then_inc(T.sem.outB, 16)
+    need("Y", [y1])
+    g.sync.dma_start(T.y[:, 128:288], T.ysb[:, 128:288]).then_inc(T.sem.outA, 16)
+    for q in ("V", "S", "T", "G"):
+        need("Y", [(q, count[q])])
+    g.sync.wait_ge(T.sem.outA, 16 * 8)
+    g.scalar.wait_ge(T.sem.outB, 16 * 2)
+    g.wait_ge(T.sem.sent, 2 * R * len(topo.engines(core, prev)))

@@ -103,6 +103,7 @@ def rank_program(g, core, T, topo):
     g.scalar.dma_start(T.ut[:, :], T.u[:, :]).then_inc(T.sem.dU, 16)
     g.scalar.dma_start(T.pin[0:1, :], T.p[:, :]).then_inc(T.sem.dP, 16)
     g.sync.dma_start(T.X0[:, 512:1152], T.x[:, 512:1152]).then_inc(T.sem.dXB, 16)
+    need("Y", [("dXA", 16)])
     g.sync.dma_start(T.wq[:, :].bitcast(dt.uint8), T.wc[:, :]).then_inc(T.sem.dW, 16)
     g.sync.dma_start(T.wsc[:, :], T.ws[:, :]).then_inc(T.sem.dW, 16)
     g.sync.dma_start(T.vt[:, :], T.v[:, :]).then_inc(T.sem.dV, 16)
@@ -128,14 +129,6 @@ def rank_program(g, core, T, topo):
     k_q = run("V", [q15], ts(col(2), T.pci[:, 2:3], -9.0, O.mult, 150.0, O.add))
     carry = [run("V", [q15], ts(T.carry[:, 0:1], T.pci[:, 2:3], -10.0, O.mult, 150.0, O.add)), 0]
     d_f = run("V", [d_and], ts(T.df[:, :], T.di[:, 32:64], 0.0, O.is_gt, -522.0, O.mult))
-    t_and = run("V", [i_t], ts(T.ti[:, 256:512], T.ti[:, 0:256], 255, O.bitwise_and))
-    d_h = run("V", [d_f], ts(T.hold[:, 0:32], T.df[:, :], 512.0, O.add))
-    t_f = run("V", [t_and], ts(T.tf[:, :], T.ti[:, 256:512], -128.0, O.add))
-    d_h = run("V", [d_h], cp(T.hold[:, 32:64], T.hold[:, 0:32]))
-    d_h = run("V", [d_h], cp(T.hold[:, 64:128], T.hold[:, 0:64]))
-    d_h = run("V", [d_h], cp(T.hold[:, 128:256], T.hold[:, 0:128]))
-    d_h = run("V", [d_h], cp(T.hold[:, 256:320], T.hold[:, 0:64]))
-    m_t = [run("S", [t_f], act(T.tab[:, 0:256], T.tf[:, :], F.Abs)), None, None, None]
     m_e = [a_e0,
            run("S", [a_e0, k_e], act(T.e1[:, :], T.e0[:, :], F.Copy, scale=col(0))),
            run("S", [a_e0, k_o], act(T.e2[:, :], T.e0[:, :], F.Copy, scale=col(1)))]
@@ -146,13 +139,21 @@ def rank_program(g, core, T, topo):
         src = (T.e0, T.e1, T.e2)[y]
         E[y, b] = run("V", [m_e[y]], quant(T.eq[:, k:k + 128], T.es[:, k:k + 128], src[:, 3 - b:515 - b]))
 
+    for b in range(4):
+        equant(0, b)
+    t_and = run("V", [i_t], ts(T.ti[:, 256:512], T.ti[:, 0:256], 255, O.bitwise_and))
+    d_h = run("V", [d_f], ts(T.hold[:, 0:32], T.df[:, :], 512.0, O.add))
+    t_f = run("V", [t_and], ts(T.tf[:, :], T.ti[:, 256:512], -128.0, O.add))
+    for b, (lo, hi) in enumerate(((32, 64), (64, 128), (128, 256), (256, 320))):
+        d_h = run("V", [d_h], cp(T.hold[:, lo:hi], T.hold[:, 0:hi - lo]))
+        equant(1, b)
+    m_t = [run("S", [t_f], act(T.tab[:, 0:256], T.tf[:, :], F.Abs)), None, None, None]
+
     def eside(y, b):
         k = 128 * (4 * y + b)
         return T.eq[:, k:k + 128], T.es[:, k:k + 128]
 
-    uq = run("V", [("dU", 16)], quant(T.uq[:, :], T.us[:, :], T.ut[:, :]))
-    u2 = [run("V", [uq, c_off0], cp(T.u2q[:, 0:128].bitcast(dt.uint32), T.uq[:, 0:128].bitcast(dt.uint32).indirect(T.off0[:, 0:8]))),
-          run("S", [uq, c_off0], act(T.u2s[:, 0:128], T.us[:, 0:128].indirect(T.off0[:, 0:8])))]
+    u2 = []
 
     QT = [T.q0, T.q1, T.q2, T.q3]
     ST = [T.s0, T.s1, T.s2, T.s3]
@@ -179,13 +180,20 @@ def rank_program(g, core, T, topo):
         S[t, k] = run("T", [qx[t, k], bank.get(bk)] + u2,
                       mm(bk, NB[k], T.u2q[:, :], T.u2s[:, :], QT[t][:, sl(k)], ST[t][:, sl(k)]))
 
-    def chain1(t, k):
+    def fill(todo):
+        if todo:
+            todo.pop(0)()
+
+    def chain1(t, k, todo=None):
         n, a = NB[k], C * t + C0[k]
         bk = 4 * k + 3
         x = run("V", [S[t, k]], ts(T.pos[:, a:a + n], T.ps[:, 512 * bk:512 * bk + n], 0.0, O.is_gt))
         bank[bk] = x
+        fill(todo)
         x = run("V", [x], scan(T.cnt[:, a:a + n], T.pos[:, a:a + n], T.pos[:, a:a + n], 0.0, O.add, O.max))
+        fill(todo)
         y = run("V", [x, d_h], scan(T.hn[:, a:a + n], T.hold[:, 0:n], T.cnt[:, a:a + n], 0.0, O.add, O.min))
+        fill(todo)
         w = 18 * t + 8 * k
         cc = carry[1]
         st[t, k, "nw"] = run("V", [y, carry[0]], ts(T.nw[:, w:w + n // 16], T.hn[:, a + 15:a + n:16], T.carry[:, cc:cc + 1], O.add))
@@ -200,10 +208,11 @@ def rank_program(g, core, T, topo):
 
     last = {}
 
-    def chain2a(t, k):
+    def chain2a(t, k, todo=None):
         n, a, d = NB[k], C * t + C0[k], 2 * (C * t + C0[k])
         x = [run("V", [st[t, k, "b"], sc[l]], ts(T.d1[:, d + l * n:d + l * n + n], T.bt[:, a:a + n], col(3 + l), O.add, col(3 + l), O.add)) for l in range(2)]
         pp = []
+        fill(todo)
         for l in range(2):
             init, tok = last.get(l, (col(3 + l), None))
             e = d + l * n
@@ -212,11 +221,14 @@ def rank_program(g, core, T, topo):
             pp.append(pt)
         st[t, k, "pl"] = pp
 
-    def chain2b(t, k):
+    def chain2b(t, k, todo=None):
         n, d, o = NB[k], 2 * (C * t + C0[k]), 36 * t + 16 * k
         m = 2 * n // 16
+        fill(todo)
         x = run("V", st[t, k, "pl"] + [d_h], scan(T.hh[:, d:d + 2 * n], T.hold[:, 0:2 * n], T.pl[:, d:d + 2 * n], 0.0, O.add, O.min))
-        x = run("V", [x] + bs, tt(T.of[:, o:o + m], T.hh[:, d + 15:d + 2 * n:16], T.base[:, 16 * k:16 * k + m], O.add))
+        fill(todo)
+        x = run("V", [x] + bs[k], tt(T.of[:, o:o + m], T.hh[:, d + 15:d + 2 * n:16], T.base[:, 16 * k:16 * k + m], O.add))
+        fill(todo)
         st[t, k, "off"] = run("V", [x], cp(T.off[:, o:o + m], T.of[:, o:o + m]))
 
     def picks(t, k):
@@ -272,34 +284,38 @@ def rank_program(g, core, T, topo):
     def yprod(k):
         n = NB[k]
         bk = 4 * k
-        x = run("T", [vq, qx[R, k], bank.get(bk)], mm(bk, n, T.vq[:, :], T.vs[:, :], T.q3[:, sl(k)], T.s3[:, sl(k)]))
-        return run("S", [x], act(T.ysb[:, sl(k)], T.ps[:, 512 * bk:512 * bk + n]))
+        return run("T", [vq, qx[R, k], bank.get(bk)], mm(bk, n, T.vq[:, :], T.vs[:, :], T.q3[:, sl(k)], T.s3[:, sl(k)]))
 
-    quantx(0, 0, [("dXA", 16)])
     pf = run("V", [("dP", 16)], cp(T.pfl[0:1, :], T.pin[0:1, :]))
-    send(0)
     pb = run("G", [pf], lambda: g.partition_broadcast(T.pbc[:, :], T.pfl[0:1, :], 128))
+    quantx(0, 0, [("dXA", 16)])
+    send(0)
+    uq = run("V", [("dU", 16)], quant(T.uq[:, :], T.us[:, :], T.ut[:, :]))
+    u2 += [run("V", [uq, c_off0], cp(T.u2q[:, 0:128].bitcast(dt.uint32), T.uq[:, 0:128].bitcast(dt.uint32).indirect(T.off0[:, 0:8]))),
+           run("S", [uq, c_off0], act(T.u2s[:, 0:128], T.us[:, 0:128].indirect(T.off0[:, 0:8])))]
     sprod(0, 0)
-    equant(0, 0)
-    equant(0, 1)
+    equant(2, 0)
+    equant(2, 1)
     chain1(0, 0)
     gath(0, 0)
-    m_t[1] = run("V", [m_t[0]], cp(T.tab[:, 256:512], T.tab[:, 0:256]))
     pm = [run("V", [pb, (a_m0, a_m1)[l]], tt(T.pm[:, 8 * l:8 * l + 8], T.pbc[:, :], T.mk[:, 8 * l:8 * l + 8], O.mult)) for l in range(2)]
+    m_t[1] = run("V", [m_t[0]], cp(T.tab[:, 256:512], T.tab[:, 0:256]))
     sc = [run("V", [pm[l]], lambda l=l: g.vector.tensor_reduce(col(3 + l), T.pm[:, 8 * l:8 * l + 8], AxisListType.X, O.add)) for l in range(2)]
-    ns = [run("V", [sc[l]], ts(col(5 + l), col(3 + l), -1.0, O.mult)) for l in range(2)]
-    cc2 = [run("V", [sc[l], k_q], tt(col(7 + l), col(2), col(3 + l), O.subtract)) for l in range(2)]
-    bs = []
-    for l in range(2):
-        bs.append(run("V", [cc2[l], i_m], ts(T.base[:, 8 * l:8 * l + 8], T.m16[:, 0:8], col(7 + l), O.add)))
-        bs.append(run("V", [cc2[l], i_m], ts(T.base[:, 16 + 10 * l:26 + 10 * l], T.m16[:, 0:10], col(7 + l), O.add)))
     quantx(0, 1, [("dXB", 16)])
-    equant(0, 2)
-    equant(0, 3)
-    chain2a(0, 0)
-    for b in range(4):
-        equant(1, b)
-    chain2b(0, 0)
+    cc2, bs = [], [[], []]
+
+    def c_cc():
+        for l in range(2):
+            cc2.append(run("V", [sc[l], k_q], tt(col(7 + l), col(2), col(3 + l), O.subtract)))
+
+    def c_base(k):
+        m = NB[k] // 16
+        for l in range(2):
+            o = 16 * k + m * l
+            bs[k].append(run("V", [cc2[l], i_m], ts(T.base[:, o:o + m], T.m16[:, 0:m], col(7 + l), O.add)))
+
+    chain2a(0, 0, [c_cc])
+    chain2b(0, 0, [lambda: c_base(0), lambda: equant(2, 2), lambda: equant(2, 3)])
     own(0, 0)
     m_t[2] = run("S", [m_t[0]], act(T.tab[:, 512:768], T.tab[:, 0:256]))
     m_t[3] = run("S", [m_t[0]], act(T.tab[:, 768:880], T.tab[:, 0:112]))
@@ -308,62 +324,66 @@ def rank_program(g, core, T, topo):
     for t in range(R):
         sprod(t, 1)
         picks(t, 0)
-        if t == 0:
-            for b in range(4):
-                equant(2, b)
         far(t, 0, 0)
         far(t, 0, 1)
-        chain1(t, 1)
-        cast(t, 0, 0)
-        gath(t, 1)
-        for b in range(1, 4):
+        chain1(t, 1, [lambda: c_base(1)] if t == 0 else None)
+        for b in range(4):
             cast(t, 0, b)
-        chain2a(t, 1)
-        qz(t, 0)
-        chain2b(t, 1)
+        gath(t, 1)
         own(t, 1)
+        qz(t, 0)
         wprod(t, 0)
-        picks(t, 1)
-        far(t, 1, 0)
-        far(t, 1, 1)
-        xupd(t, 0, range(4))
+        xs = [lambda b=b: xupd(t, 0, (b,)) for b in range(4)]
+        chain2a(t, 1, xs)
+        chain2b(t, 1, xs)
+        for f in xs:
+            f()
         newx(t, 0)
         if t < R - 1:
             send(t + 1)
-        for b in range(4):
-            cast(t, 1, b)
-        if t < R - 1:
+            picks(t, 1)
             sprod(t + 1, 0)
-        qz(t, 1)
-        wprod(t, 1)
-        if t < R - 1:
+            far(t, 1, 0)
+            far(t, 1, 1)
             chain1(t + 1, 0)
             gath(t + 1, 0)
+            chain2a(t + 1, 0)
+            chain2b(t + 1, 0)
+            for b in range(4):
+                cast(t, 1, b)
+            qz(t, 1)
+            wprod(t, 1)
             if t == 0:
                 vq = run("V", [("dV", 16)], quant(T.vq[:, :], T.vs[:, :], T.vt[:, :]))
-            xupd(t, 1, range(2))
-            chain2a(t + 1, 0)
-            xupd(t, 1, range(2, 4))
-            chain2b(t + 1, 0)
+            xupd(t, 1, range(4))
             newx(t, 1)
             own(t + 1, 0)
         else:
+            picks(t, 1)
+            far(t, 1, 0)
+            far(t, 1, 1)
             y0 = yprod(0)
-            need("Y", [qx[R, 0]])
-            g.sync.dma_start(T.oc[:, 0:512], T.q3[:, 0:128].bitcast(dt.uint8)).then_inc(T.sem.outA, 16)
-            need("Y", [y0])
-            g.sync.dma_start(T.y[:, 0:128], T.ysb[:, 0:128]).then_inc(T.sem.outA, 16)
+            for b in range(4):
+                cast(t, 1, b)
+            ns = [run("V", [sc[l]], ts(col(5 + l), col(3 + l), -1.0, O.mult)) for l in range(2)]
             ax = []
             for kk in range(2):
                 n, d = NB[kk], 2 * (C * t + C0[kk])
                 for l in range(2):
                     ax.append(run("S", st[t, kk, "pl"] + [ns[l]], act((T.ao0, T.ao1)[l][:, sl(kk)], T.pl[:, d + l * n:d + l * n + n], F.Identity, bias=col(5 + l))))
+            ys = run("S", [y0], act(T.ysb[:, 0:128], T.ps[:, 0:128]))
+            need("Y", [qx[R, 0]])
+            g.sync.dma_start(T.oc[:, 0:512], T.q3[:, 0:128].bitcast(dt.uint8)).then_inc(T.sem.outA, 16)
             need("Y", ax)
             for l in range(2):
                 g.sync.dma_start(T.ao[l:8:2, :], (T.ao0, T.ao1)[l][0:128:32, :]).then_inc(T.sem.outA, 16)
+            need("Y", [ys])
+            g.sync.dma_start(T.y[:, 0:128], T.ysb[:, 0:128]).then_inc(T.sem.outA, 16)
+            qz(t, 1)
+            wprod(t, 1)
             xupd(t, 1, range(4))
             newx(t, 1)
-    y1 = yprod(1)
+    y1 = run("S", [yprod(1)], act(T.ysb[:, 128:288], T.ps[:, 2048:2208]))
     need("Y", [qx[R, 1]])
     for k in range(3):
         g.sync.dma_start(T.osc[4 * k:4 * k + 4, :], T.s3[32 * k:32 * k + 4, 0:C]).then_inc(T.sem.outA, 16)

@@ -5,6 +5,7 @@ C, H, R, W = 288, 128, 3, 416
 C0 = (0, 128)
 NB = (128, 160)
 TAB = 880
+VC = ((), (1, 3))
 
 F8 = "float8_e4m3fn_x4"
 SCRATCH = {
@@ -21,7 +22,7 @@ SCRATCH = {
     "off0": ("sbuf", [128, 8], "uint16"),
     "pci": ("sbuf", [128, 4], "int32"), "pcf": ("sbuf", [128, 16], "float32"),
     "di": ("sbuf", [128, 64], "int32"), "df": ("sbuf", [128, 32], "float32"), "hold": ("sbuf", [128, 320], "bfloat16"),
-    "ti": ("sbuf", [128, 512], "int32"), "tf": ("sbuf", [128, 256], "float32"), "tab": ("sbuf", [128, TAB], "bfloat16"),
+    "tf": ("sbuf", [128, 1280], "float32"), "tab": ("sbuf", [128, TAB], "bfloat16"),
     "m16": ("sbuf", [128, 10], "float32"), "base": ("sbuf", [128, 36], "float32"),
     "one8": ("sbuf", [128, 8], "float32"), "mk": ("sbuf", [128, 16], "float32"),
     "pin": ("sbuf", [1, 8], "int32"), "pfl": ("sbuf", [1, 8], "float32"), "pbc": ("sbuf", [128, 8], "float32"),
@@ -100,8 +101,8 @@ def rank_program(g, core, T, topo):
         return lambda: g.tensor.matmul_mx(T.ps[:, 512 * bank:512 * bank + n], lq, ls, rq, rs, start, stop)
 
     g.sync.dma_start(T.X0[:, 0:512], T.x[:, 0:512]).then_inc(T.sem.dXA, 16)
-    g.scalar.dma_start(T.ut[:, :], T.u[:, :]).then_inc(T.sem.dU, 16)
     g.scalar.dma_start(T.pin[0:1, :], T.p[:, :]).then_inc(T.sem.dP, 16)
+    g.sync.dma_start(T.ut[:, :], T.u[:, :]).then_inc(T.sem.dU, 16)
     g.sync.dma_start(T.X0[:, 512:1152], T.x[:, 512:1152]).then_inc(T.sem.dXB, 16)
     need("Y", [("dXA", 16)])
     g.sync.dma_start(T.wq[:, :].bitcast(dt.uint8), T.wc[:, :]).then_inc(T.sem.dW, 16)
@@ -113,9 +114,9 @@ def rank_program(g, core, T, topo):
     c_off0 = run("V", [], lambda: g.vector.memset(T.off0[:, :], 0))
     c_one = run("V", [], lambda: g.vector.memset(T.one8[:, :], 1.0))
     i_p = run("G", [], lambda: g.iota(T.pci[:, 0:1], [[0, 1]], 0, 1))
+    i_t = run("G", [], lambda: g.iota(T.tf[:, 0:256], [[9, 256]], 0, 0, allow_small_or_imprecise_dtypes=True))
     i_d = run("G", [], lambda: g.iota(T.di[:, 0:32], [[1, 32]], 128, -1))
     a_e0 = run("G", [c_cst, c_e0], lambda: g.affine_select(T.e0[:, 3:515:4], T.cst[:, :], [[-1, 128]], O.is_equal, 0.0, 0, 1))
-    i_t = run("G", [], lambda: g.iota(T.ti[:, 0:256], [[9, 256]], 0, 0))
     i_m = run("G", [], lambda: g.iota(T.m16[:, :], [[16, 10]], 0, 0, allow_small_or_imprecise_dtypes=True))
     a_m0 = run("G", [c_one], lambda: g.affine_select(T.mk[:, 0:8], T.one8[:, :], [[-32, 4], [-32, 2]], O.is_ge, 0.0, 0, 1))
     a_m1 = run("G", [c_one], lambda: g.affine_select(T.mk[:, 8:16], T.one8[:, :], [[-32, 4], [0, 2]], O.is_ge, 0.0, 0, 1))
@@ -130,8 +131,8 @@ def rank_program(g, core, T, topo):
     carry = [run("V", [q15], ts(T.carry[:, 0:1], T.pci[:, 2:3], -10.0, O.mult, 150.0, O.add)), 0]
     d_f = run("V", [d_and], ts(T.df[:, :], T.di[:, 32:64], 0.0, O.is_gt, -522.0, O.mult))
     m_e = [a_e0,
-           run("S", [a_e0, k_e], act(T.e1[:, :], T.e0[:, :], F.Copy, scale=col(0))),
-           run("S", [a_e0, k_o], act(T.e2[:, :], T.e0[:, :], F.Copy, scale=col(1)))]
+           run("V", [a_e0, k_e], ts(T.e1[:, :], T.e0[:, :], col(0), O.mult)),
+           run("V", [a_e0, k_o], ts(T.e2[:, :], T.e0[:, :], col(1), O.mult))]
     E = {}
 
     def equant(y, b):
@@ -141,13 +142,15 @@ def rank_program(g, core, T, topo):
 
     for b in range(4):
         equant(0, b)
-    t_and = run("V", [i_t], ts(T.ti[:, 256:512], T.ti[:, 0:256], 255, O.bitwise_and))
-    d_h = run("V", [d_f], ts(T.hold[:, 0:32], T.df[:, :], 512.0, O.add))
-    t_f = run("V", [t_and], ts(T.tf[:, :], T.ti[:, 256:512], -128.0, O.add))
-    for b, (lo, hi) in enumerate(((32, 64), (64, 128), (128, 256), (256, 320))):
-        d_h = run("V", [d_h], cp(T.hold[:, lo:hi], T.hold[:, 0:hi - lo]))
-        equant(1, b)
-    m_t = [run("S", [t_f], act(T.tab[:, 0:256], T.tf[:, :], F.Abs)), None, None, None]
+    for i, c in enumerate((1280.0, 768.0, 512.0, 256.0)):
+        i_t = run("S", [i_t], act(T.tf[:, 256 * i + 256:256 * i + 512], T.tf[:, 256 * i:256 * i + 256], F.Abs, bias=-c))
+        if i == 0:
+            d_h = run("S", [d_f], act(T.hold[:, 0:32], T.df[:, :], F.Identity, bias=512.0))
+        else:
+            lo = 16 << i
+            d_h = run("S", [d_h], act(T.hold[:, lo:2 * lo], T.hold[:, 0:lo]))
+    m_t = [run("S", [i_t], act(T.tab[:, 0:256], T.tf[:, 1024:1280], F.Abs, bias=-128.0))]
+    d_h = run("S", [d_h], act(T.hold[:, 256:320], T.hold[:, 0:64]))
 
     def eside(y, b):
         k = 128 * (4 * y + b)
@@ -171,7 +174,7 @@ def rank_program(g, core, T, topo):
     def send(t):
         need("G", [qx[t, 0]])
         rid, pid = topo.addr(prev, core)
-        m = topo.mask(core, prev)
+        m = sum(1 << e for e in topo.engines(core, prev)[::2])
         g.remote_dma(QT[t][:, C:W].bitcast(dt.uint8), QT[t][:, 0:H].bitcast(dt.uint8), T.sem["arr%d" % t], T.sem.sent, pid, rid, m)
         g.remote_dma(ST[t][:, C:W], ST[t][:, 0:H], T.sem["arr%d" % t], T.sem.sent, pid, rid, m)
 
@@ -197,14 +200,19 @@ def rank_program(g, core, T, topo):
         w = 18 * t + 8 * k
         cc = carry[1]
         st[t, k, "nw"] = run("V", [y, carry[0]], ts(T.nw[:, w:w + n // 16], T.hn[:, a + 15:a + n:16], T.carry[:, cc:cc + 1], O.add))
-        carry[0] = run("V", [x, carry[0]], tt(T.carry[:, cc + 1:cc + 2], T.carry[:, cc:cc + 1], T.cnt[:, a + n - 1:a + n], O.add))
-        carry[1] = cc + 1
+        st[t, k, "last"] = (x, T.cnt[:, a + n - 1:a + n])
 
     def gath(t, k):
         n, a, w = NB[k], C * t + C0[k], 18 * t + 8 * k
         width = (256, 512)[k] if t == 0 else TAB
         st[t, k, "b"] = run("S", [st[t, k, "nw"]] + m_t[:1 if width == 256 else 2 if width == 512 else 4],
                             act(T.bt[:, a:a + n], T.tab[:, 0:width].indirect(T.nw[:, w:w + n // 16])))
+
+    def count_on(t, k):
+        x, e = st[t, k, "last"]
+        cc = carry[1]
+        carry[0] = run("S", [x, carry[0]], act(T.carry[:, cc + 1:cc + 2], e, F.Identity, bias=T.carry[:, cc:cc + 1]))
+        carry[1] = cc + 1
 
     last = {}
 
@@ -235,7 +243,7 @@ def rank_program(g, core, T, topo):
         n, o = NB[k], 36 * t + 16 * k
         lo, hi = (0, C) if k == 0 else (H, W)
         fq, fs = T["f%d%d" % (t, k)], T["g%d%d" % (t, k)]
-        deps = [st[t, k, "off"], qx[t, 0], qx[t, 1]] + ([("arr%d" % t, 2 * len(topo.engines(nxt, core)))] if k else [])
+        deps = [st[t, k, "off"], qx[t, 0], qx[t, 1]] + ([("arr%d" % t, 2 * len(topo.engines(nxt, core)[::2]))] if k else [])
         for l in range(2):
             off = T.off[:, o + l * n // 16:o + (l + 1) * n // 16]
             c, d = l * n, (l + 1) * n
@@ -243,8 +251,8 @@ def rank_program(g, core, T, topo):
                 run("V", deps, cp(fq[:, c:d].bitcast(dt.uint32), QT[t][:, lo:hi].bitcast(dt.uint32).indirect(off))),
                 run("S", deps, act(fs[:, c:d], ST[t][:, lo:hi].indirect(off)))]
 
-    def own(t, k):
-        for b in range(4):
+    def own(t, k, bs_=range(4)):
+        for b in bs_:
             bk = 4 * k + b
             lq, ls = eside(0, b)
             run("T", [E[0, b], qx[t, k], bank.get(bk)], mm(bk, NB[k], lq, ls, QT[t][:, sl(k)], ST[t][:, sl(k)], True, False))
@@ -257,9 +265,17 @@ def rank_program(g, core, T, topo):
             st[t, k, "z", b] = run("T", [E[1 + l, b]] + st[t, k, "pk", l],
                                    mm(4 * k + b, n, lq, ls, fq[:, l * n:l * n + n], fs[:, l * n:l * n + n], False, l == 1))
 
+    def on_v(k):
+        return VC[k]
+
+    def on_s(k):
+        return [b for b in range(4) if b not in VC[k]]
+
     def cast(t, k, b):
         n, z = NB[k], 4 * (C * t + C0[k])
-        st[t, k, "c", b] = bank[4 * k + b] = run("S", [st[t, k, "z", b]], act(T.zt[:, z + b:z + 4 * n:4], T.ps[:, 512 * (4 * k + b):512 * (4 * k + b) + n]))
+        out, in_ = T.zt[:, z + b:z + 4 * n:4], T.ps[:, 512 * (4 * k + b):512 * (4 * k + b) + n]
+        v = b in on_v(k)
+        st[t, k, "c", b] = bank[4 * k + b] = run("V" if v else "S", [st[t, k, "z", b]], cp(out, in_) if v else act(out, in_))
 
     def qz(t, k):
         n, a = NB[k], C * t + C0[k]
@@ -294,12 +310,14 @@ def rank_program(g, core, T, topo):
     u2 += [run("V", [uq, c_off0], cp(T.u2q[:, 0:128].bitcast(dt.uint32), T.uq[:, 0:128].bitcast(dt.uint32).indirect(T.off0[:, 0:8]))),
            run("S", [uq, c_off0], act(T.u2s[:, 0:128], T.us[:, 0:128].indirect(T.off0[:, 0:8])))]
     sprod(0, 0)
-    equant(2, 0)
-    equant(2, 1)
-    chain1(0, 0)
+    equant(1, 0)
+    equant(1, 1)
+    chain1(0, 0, [lambda: equant(1, 2), lambda: equant(1, 3)])
     gath(0, 0)
+    count_on(0, 0)
+    for lo, hi in ((256, 512), (512, 768), (768, TAB)):
+        m_t.append(run("S", m_t[:1], act(T.tab[:, lo:hi], T.tab[:, 0:hi - lo])))
     pm = [run("V", [pb, (a_m0, a_m1)[l]], tt(T.pm[:, 8 * l:8 * l + 8], T.pbc[:, :], T.mk[:, 8 * l:8 * l + 8], O.mult)) for l in range(2)]
-    m_t[1] = run("V", [m_t[0]], cp(T.tab[:, 256:512], T.tab[:, 0:256]))
     sc = [run("V", [pm[l]], lambda l=l: g.vector.tensor_reduce(col(3 + l), T.pm[:, 8 * l:8 * l + 8], AxisListType.X, O.add)) for l in range(2)]
     quantx(0, 1, [("dXB", 16)])
     cc2, bs = [], [[], []]
@@ -315,24 +333,29 @@ def rank_program(g, core, T, topo):
             bs[k].append(run("V", [cc2[l], i_m], ts(T.base[:, o:o + m], T.m16[:, 0:m], col(7 + l), O.add)))
 
     chain2a(0, 0, [c_cc])
-    chain2b(0, 0, [lambda: c_base(0), lambda: equant(2, 2), lambda: equant(2, 3)])
+    chain2b(0, 0, [lambda: c_base(0), lambda: equant(2, 0), lambda: equant(2, 1)])
     own(0, 0)
-    m_t[2] = run("S", [m_t[0]], act(T.tab[:, 512:768], T.tab[:, 0:256]))
-    m_t[3] = run("S", [m_t[0]], act(T.tab[:, 768:880], T.tab[:, 0:112]))
     vq = None
 
     for t in range(R):
         sprod(t, 1)
         picks(t, 0)
         far(t, 0, 0)
+        if t == 0:
+            equant(2, 2)
+            equant(2, 3)
         far(t, 0, 1)
-        chain1(t, 1, [lambda: c_base(1)] if t == 0 else None)
-        for b in range(4):
+        for b in on_s(0):
             cast(t, 0, b)
+        chain1(t, 1, [lambda: None] + [lambda b=b: cast(t, 0, b) for b in on_v(0)])
         gath(t, 1)
-        own(t, 1)
+        count_on(t, 1)
+        own(t, 1, (0, 1))
         qz(t, 0)
         wprod(t, 0)
+        own(t, 1, (2, 3))
+        if t == 0:
+            c_base(1)
         xs = [lambda b=b: xupd(t, 0, (b,)) for b in range(4)]
         chain2a(t, 1, xs)
         chain2b(t, 1, xs)
@@ -347,25 +370,31 @@ def rank_program(g, core, T, topo):
             far(t, 1, 1)
             chain1(t + 1, 0)
             gath(t + 1, 0)
-            chain2a(t + 1, 0)
-            chain2b(t + 1, 0)
-            for b in range(4):
+            for b in on_s(1) + list(on_v(1)[:-1]):
                 cast(t, 1, b)
-            qz(t, 1)
+            count_on(t + 1, 0)
+
+            def zb():
+                for b in on_v(1)[-1:]:
+                    cast(t, 1, b)
+                qz(t, 1)
+            chain2a(t + 1, 0, [zb])
             wprod(t, 1)
-            if t == 0:
-                vq = run("V", [("dV", 16)], quant(T.vq[:, :], T.vs[:, :], T.vt[:, :]))
-            xupd(t, 1, range(4))
+            xs = [lambda b=b: xupd(t, 1, (b,)) for b in range(4)]
+            chain2b(t + 1, 0, [lambda: None] + xs)
+            for b in range(2, 4):
+                xs[b]()
             newx(t, 1)
             own(t + 1, 0)
         else:
             picks(t, 1)
             far(t, 1, 0)
             far(t, 1, 1)
+            vq = run("V", [("dV", 16)], quant(T.vq[:, :], T.vs[:, :], T.vt[:, :]))
+            ns = [run("V", [sc[l]], ts(col(5 + l), col(3 + l), -1.0, O.mult)) for l in range(2)]
             y0 = yprod(0)
             for b in range(4):
                 cast(t, 1, b)
-            ns = [run("V", [sc[l]], ts(col(5 + l), col(3 + l), -1.0, O.mult)) for l in range(2)]
             ax = []
             for kk in range(2):
                 n, d = NB[kk], 2 * (C * t + C0[kk])
@@ -395,4 +424,4 @@ def rank_program(g, core, T, topo):
         need("Y", [(q, count[q])])
     g.sync.wait_ge(T.sem.outA, 16 * 8)
     g.scalar.wait_ge(T.sem.outB, 16 * 2)
-    g.wait_ge(T.sem.sent, 2 * R * len(topo.engines(core, prev)))
+    g.wait_ge(T.sem.sent, 2 * R * len(topo.engines(core, prev)[::2]))

from concourse.bass import DstId, RemoteDMATransfer
from concourse.mybir import dt, AluOpType as O, AxisListType, ActivationFunctionType as F

C, H, R, W = 288, 128, 3, 416
C0 = (0, 128)
NB = (128, 160)
TAB = 880
VC = ((), (1, 3))

F8 = "float8_e4m3fn_x4"
SCRATCH = {
    "X0": ("sbuf", [128, 4 * C], "bfloat16"), "X1": ("sbuf", [128, 4 * C], "bfloat16"),
    "X2": ("sbuf", [128, 4 * C], "bfloat16"), "X3": ("sbuf", [128, 4 * C], "bfloat16"),
    "ut": ("sbuf", [128, 512], "bfloat16"), "vt": ("sbuf", [128, 512], "bfloat16"),
    "uq": ("sbuf", [128, 128], F8), "us": ("sbuf", [128, 128], "uint8"),
    "u2q": ("sbuf", [128, 128], F8), "u2s": ("sbuf", [128, 128], "uint8"),
    "vq": ("sbuf", [128, 128], F8), "vs": ("sbuf", [128, 128], "uint8"),
    "wq": ("sbuf", [128, 512], F8), "wsc": ("sbuf", [128, 512], "uint8"),
    "cst": ("sbuf", [128, 128], "bfloat16"),
    "e0": ("sbuf", [128, 516], "bfloat16"), "e1": ("sbuf", [128, 516], "bfloat16"), "e2": ("sbuf", [128, 516], "bfloat16"),
    "eq": ("sbuf", [128, 1536], F8), "es": ("sbuf", [128, 1536], "uint8"),
    "off0": ("sbuf", [128, 8], "uint16"),
    "pci": ("sbuf", [128, 4], "int32"), "pcf": ("sbuf", [128, 16], "float32"),
    "di": ("sbuf", [128, 64], "int32"), "df": ("sbuf", [128, 32], "float32"), "hold": ("sbuf", [128, 320], "bfloat16"),
    "tf": ("sbuf", [128, 1280], "float32"), "tab": ("sbuf", [128, TAB], "bfloat16"),
    "m16": ("sbuf", [128, 10], "float32"), "base": ("sbuf", [128, 36], "float32"),
    "one8": ("sbuf", [128, 8], "float32"), "mk": ("sbuf", [128, 16], "float32"),
    "pin": ("sbuf", [1, 8], "int32"), "pfl": ("sbuf", [1, 8], "float32"), "pbc": ("sbuf", [128, 8], "float32"),
    "pm": ("sbuf", [128, 16], "float32"),
    "carry": ("sbuf", [128, 16], "float32"),
    "pos": ("sbuf", [128, R * C], "bfloat16"), "cnt": ("sbuf", [128, R * C], "bfloat16"),
    "hn": ("sbuf", [128, R * C], "bfloat16"), "bt": ("sbuf", [128, R * C], "bfloat16"),
    "nw": ("sbuf", [128, R * 18], "uint16"),
    "d1": ("sbuf", [128, R * 2 * C], "bfloat16"), "pl": ("sbuf", [128, R * 2 * C], "bfloat16"),
    "hh": ("sbuf", [128, R * 2 * C], "bfloat16"),
    "of": ("sbuf", [128, R * 36], "float32"), "off": ("sbuf", [128, R * 36], "uint16"),
    "zt": ("sbuf", [128, R * 4 * C], "bfloat16"),
    "zq": ("sbuf", [128, R * C], F8), "zs": ("sbuf", [128, R * C], "uint8"),
    "ysb": ("sbuf", [128, C], "float32"), "ao0": ("sbuf", [128, C], "float32"), "ao1": ("sbuf", [128, C], "float32"),
    "ps": ("psum", [128, 4096], "float32"),
}
for _t in range(R + 1):
    SCRATCH["q%d" % _t] = ("sbuf", [128, W], F8)
    SCRATCH["s%d" % _t] = ("sbuf", [128, W], "uint8")
for _t in range(R):
    for _k in range(2):
        SCRATCH["f%d%d" % (_t, _k)] = ("sbuf", [128, 2 * NB[_k]], F8)
        SCRATCH["g%d%d" % (_t, _k)] = ("sbuf", [128, 2 * NB[_k]], "uint8")
SEMAPHORES = ["V", "S", "T", "G", "dXA", "dXB", "dU", "dP", "dW", "dV", "arr0", "arr1", "arr2", "sent", "outA", "outB"]


def rank_program(g, core, T, topo):
    rank = T.rank_of(core)
    if rank is None:
        return
    n_ranks = len(T.cores)
    prev = T.cores[(rank - 1) % n_ranks]
    nxt = T.cores[(rank + 1) % n_ranks]
    eng = {"V": g.vector, "S": g.scalar, "T": g.tensor, "G": g, "Y": g.sync}
    count = {"V": 0, "S": 0, "T": 0, "G": 0}
    known = {}

    def need(q, toks):
        best = {}
        for tk in toks:
            if tk is None:
                continue
            best[tk[0]] = max(best.get(tk[0], 0), tk[1])
        for s in best:
            if best[s] > known.get((q, s), 0):
                eng[q].wait_ge(T.sem[s], best[s])
                known[(q, s)] = best[s]

    def run(q, deps, call):
        need(q, deps)
        call().then_inc(T.sem[q], 1)
        count[q] += 1
        return (q, count[q])

    def ts(out, in0, s1, op0, s2=None, op1=None):
        if op1 is None:
            return lambda: g.vector.tensor_scalar(out, in0, s1, None, op0)
        return lambda: g.vector.tensor_scalar(out, in0, s1, s2, op0, op1)

    def tt(out, a, b, op):
        return lambda: g.vector.tensor_tensor(out, a, b, op)

    def cp(out, in_):
        return lambda: g.vector.tensor_copy(out, in_)

    def scan(out, d0, d1, init, op0, op1):
        return lambda: g.vector.tensor_tensor_scan(out, d0, d1, init, op0, op1)

    def act(out, in_, f=F.Copy, **kw):
        return lambda: g.scalar.activation(out, in_, f, **kw)

    def quant(q, s, t):
        return lambda: g.vector.quantize_mx(q, s, t)

    def mm(bank, n, lq, ls, rq, rs, start=True, stop=True):
        return lambda: g.tensor.matmul_mx(T.ps[:, 512 * bank:512 * bank + n], lq, ls, rq, rs, start, stop)

    g.sync.dma_start(T.X0[:, 0:512], T.x[:, 0:512]).then_inc(T.sem.dXA, 16)
    g.scalar.dma_start(T.pin[0:1, :], T.p[:, :]).then_inc(T.sem.dP, 16)
    g.sync.dma_start(T.ut[:, :], T.u[:, :]).then_inc(T.sem.dU, 16)
    g.sync.dma_start(T.X0[:, 512:1152], T.x[:, 512:1152]).then_inc(T.sem.dXB, 16)
    need("Y", [("dXA", 16)])
    g.sync.dma_start(T.wq[:, :].bitcast(dt.uint8), T.wc[:, :]).then_inc(T.sem.dW, 16)
    g.sync.dma_start(T.wsc[:, :], T.ws[:, :]).then_inc(T.sem.dW, 16)
    g.sync.dma_start(T.vt[:, :], T.v[:, :]).then_inc(T.sem.dV, 16)

    c_cst = run("V", [], lambda: g.vector.memset(T.cst[:, :], 2.0 ** -6))
    c_e0 = run("V", [], lambda: g.vector.memset(T.e0[:, :], 0.0))
    c_off0 = run("V", [], lambda: g.vector.memset(T.off0[:, :], 0))
    c_one = run("V", [], lambda: g.vector.memset(T.one8[:, :], 1.0))
    i_p = run("G", [], lambda: g.iota(T.pci[:, 0:1], [[0, 1]], 0, 1))
    i_t = run("G", [], lambda: g.iota(T.tf[:, 0:256], [[9, 256]], 0, 0, allow_small_or_imprecise_dtypes=True))
    i_d = run("G", [], lambda: g.iota(T.di[:, 0:32], [[1, 32]], 128, -1))
    a_e0 = run("G", [c_cst, c_e0], lambda: g.affine_select(T.e0[:, 3:515:4], T.cst[:, :], [[-1, 128]], O.is_equal, 0.0, 0, 1))
    i_m = run("G", [], lambda: g.iota(T.m16[:, :], [[16, 10]], 0, 0, allow_small_or_imprecise_dtypes=True))
    a_m0 = run("G", [c_one], lambda: g.affine_select(T.mk[:, 0:8], T.one8[:, :], [[-32, 4], [-32, 2]], O.is_ge, 0.0, 0, 1))
    a_m1 = run("G", [c_one], lambda: g.affine_select(T.mk[:, 8:16], T.one8[:, :], [[-32, 4], [0, 2]], O.is_ge, 0.0, 0, 1))

    col = lambda k: T.pcf[:, k:k + 1]
    h = run("V", [i_p], ts(T.pci[:, 1:2], T.pci[:, 0:1], 16, O.bitwise_and))
    q15 = run("V", [i_p], ts(T.pci[:, 2:3], T.pci[:, 0:1], 15, O.bitwise_and))
    d_and = run("V", [i_d], ts(T.di[:, 32:64], T.di[:, 0:32], 15, O.bitwise_and))
    k_e = run("V", [h], ts(col(0), T.pci[:, 1:2], 0.0, O.is_equal))
    k_o = run("V", [h], ts(col(1), T.pci[:, 1:2], 0.0, O.is_gt))
    k_q = run("V", [q15], ts(col(2), T.pci[:, 2:3], -9.0, O.mult, 150.0, O.add))
    carry = [run("V", [q15], ts(T.carry[:, 0:1], T.pci[:, 2:3], -10.0, O.mult, 150.0, O.add)), 0]
    d_f = run("V", [d_and], ts(T.df[:, :], T.di[:, 32:64], 0.0, O.is_gt, -522.0, O.mult))
    m_e = [a_e0,
           run("V", [a_e0, k_e], ts(T.e1[:, :], T.e0[:, :], col(0), O.mult)),
           run("V", [a_e0, k_o], ts(T.e2[:, :], T.e0[:, :], col(1), O.mult))]
    E = {}

    def equant(y, b):
        k = 128 * (4 * y + b)
        src = (T.e0, T.e1, T.e2)[y]
        E[y, b] = run("V", [m_e[y]], quant(T.eq[:, k:k + 128], T.es[:, k:k + 128], src[:, 3 - b:515 - b]))

    for b in range(4):
        equant(0, b)
    for i, c in enumerate((1280.0, 768.0, 512.0, 256.0)):
        i_t = run("S", [i_t], act(T.tf[:, 256 * i + 256:256 * i + 512], T.tf[:, 256 * i:256 * i + 256], F.Abs, bias=-c))
        if i == 0:
            d_h = run("S", [d_f], act(T.hold[:, 0:32], T.df[:, :], F.Identity, bias=512.0))
        else:
            lo = 16 << i
            d_h = run("S", [d_h], act(T.hold[:, lo:2 * lo], T.hold[:, 0:lo]))
    m_t = [run("S", [i_t], act(T.tab[:, 0:256], T.tf[:, 1024:1280], F.Abs, bias=-128.0))]
    d_h = run("S", [d_h], act(T.hold[:, 256:320], T.hold[:, 0:64]))

    def eside(y, b):
        k = 128 * (4 * y + b)
        return T.eq[:, k:k + 128], T.es[:, k:k + 128]

    u2 = []

    QT = [T.q0, T.q1, T.q2, T.q3]
    ST = [T.s0, T.s1, T.s2, T.s3]
    XT = [T.X0, T.X1, T.X2, T.X3]
    bank = {}
    qx, S, st = {}, {}, {}

    def sl(k):
        return slice(C0[k], C0[k] + NB[k])

    def quantx(t, k, deps):
        a, n = C0[k], NB[k]
        qx[t, k] = run("V", deps, quant(QT[t][:, a:a + n], ST[t][:, a:a + n], XT[t][:, 4 * a:4 * a + 4 * n]))

    def send(t):
        need("G", [qx[t, 0]])
        rid, pid = topo.addr(prev, core)
        m = sum(1 << e for e in topo.engines(core, prev)[::2])
        g.remote_dma(QT[t][:, C:W].bitcast(dt.uint8), QT[t][:, 0:H].bitcast(dt.uint8), T.sem["arr%d" % t], T.sem.sent, pid, rid, m)
        g.remote_dma(ST[t][:, C:W], ST[t][:, 0:H], T.sem["arr%d" % t], T.sem.sent, pid, rid, m)

    def sprod(t, k):
        bk = 4 * k + 3
        S[t, k] = run("T", [qx[t, k], bank.get(bk)] + u2,
                      mm(bk, NB[k], T.u2q[:, :], T.u2s[:, :], QT[t][:, sl(k)], ST[t][:, sl(k)]))

    def fill(todo):
        if todo:
            todo.pop(0)()

    def chain1(t, k, todo=None):
        n, a = NB[k], C * t + C0[k]
        bk = 4 * k + 3
        x = run("V", [S[t, k]], ts(T.pos[:, a:a + n], T.ps[:, 512 * bk:512 * bk + n], 0.0, O.is_gt))
        bank[bk] = x
        fill(todo)
        x = run("V", [x], scan(T.cnt[:, a:a + n], T.pos[:, a:a + n], T.pos[:, a:a + n], 0.0, O.add, O.max))
        fill(todo)
        y = run("V", [x, d_h], scan(T.hn[:, a:a + n], T.hold[:, 0:n], T.cnt[:, a:a + n], 0.0, O.add, O.min))
        fill(todo)
        w = 18 * t + 8 * k
        cc = carry[1]
        st[t, k, "nw"] = run("V", [y, carry[0]], ts(T.nw[:, w:w + n // 16], T.hn[:, a + 15:a + n:16], T.carry[:, cc:cc + 1], O.add))
        st[t, k, "last"] = (x, T.cnt[:, a + n - 1:a + n])

    def gath(t, k):
        n, a, w = NB[k], C * t + C0[k], 18 * t + 8 * k
        width = (256, 512)[k] if t == 0 else TAB
        st[t, k, "b"] = run("S", [st[t, k, "nw"]] + m_t[:1 if width == 256 else 2 if width == 512 else 4],
                            act(T.bt[:, a:a + n], T.tab[:, 0:width].indirect(T.nw[:, w:w + n // 16])))

    def count_on(t, k):
        x, e = st[t, k, "last"]
        cc = carry[1]
        carry[0] = run("S", [x, carry[0]], act(T.carry[:, cc + 1:cc + 2], e, F.Identity, bias=T.carry[:, cc:cc + 1]))
        carry[1] = cc + 1

    last = {}

    def chain2a(t, k, todo=None):
        n, a, d = NB[k], C * t + C0[k], 2 * (C * t + C0[k])
        x = [run("V", [st[t, k, "b"], sc[l]], ts(T.d1[:, d + l * n:d + l * n + n], T.bt[:, a:a + n], col(3 + l), O.add, col(3 + l), O.add)) for l in range(2)]
        pp = []
        fill(todo)
        for l in range(2):
            init, tok = last.get(l, (col(3 + l), None))
            e = d + l * n
            pt = run("V", [x[l], st[t, k, "b"], tok], scan(T.pl[:, e:e + n], T.bt[:, a:a + n], T.d1[:, e:e + n], init, O.max, O.min))
            last[l] = (T.pl[:, e + n - 1:e + n], pt)
            pp.append(pt)
        st[t, k, "pl"] = pp

    def chain2b(t, k, todo=None):
        n, d, o = NB[k], 2 * (C * t + C0[k]), 36 * t + 16 * k
        m = 2 * n // 16
        fill(todo)
        x = run("V", st[t, k, "pl"] + [d_h], scan(T.hh[:, d:d + 2 * n], T.hold[:, 0:2 * n], T.pl[:, d:d + 2 * n], 0.0, O.add, O.min))
        fill(todo)
        x = run("V", [x] + bs[k], tt(T.of[:, o:o + m], T.hh[:, d + 15:d + 2 * n:16], T.base[:, 16 * k:16 * k + m], O.add))
        fill(todo)
        st[t, k, "off"] = run("V", [x], cp(T.off[:, o:o + m], T.of[:, o:o + m]))

    def picks(t, k):
        n, o = NB[k], 36 * t + 16 * k
        lo, hi = (0, C) if k == 0 else (H, W)
        fq, fs = T["f%d%d" % (t, k)], T["g%d%d" % (t, k)]
        deps = [st[t, k, "off"], qx[t, 0], qx[t, 1]] + ([("arr%d" % t, 2 * len(topo.engines(nxt, core)[::2]))] if k else [])
        for l in range(2):
            off = T.off[:, o + l * n // 16:o + (l + 1) * n // 16]
            c, d = l * n, (l + 1) * n
            st[t, k, "pk", l] = [
                run("V", deps, cp(fq[:, c:d].bitcast(dt.uint32), QT[t][:, lo:hi].bitcast(dt.uint32).indirect(off))),
                run("S", deps, act(fs[:, c:d], ST[t][:, lo:hi].indirect(off)))]

    def own(t, k, bs_=range(4)):
        for b in bs_:
            bk = 4 * k + b
            lq, ls = eside(0, b)
            run("T", [E[0, b], qx[t, k], bank.get(bk)], mm(bk, NB[k], lq, ls, QT[t][:, sl(k)], ST[t][:, sl(k)], True, False))

    def far(t, k, l):
        n = NB[k]
        fq, fs = T["f%d%d" % (t, k)], T["g%d%d" % (t, k)]
        for b in range(4):
            lq, ls = eside(1 + l, b)
            st[t, k, "z", b] = run("T", [E[1 + l, b]] + st[t, k, "pk", l],
                                   mm(4 * k + b, n, lq, ls, fq[:, l * n:l * n + n], fs[:, l * n:l * n + n], False, l == 1))

    def on_v(k):
        return VC[k]

    def on_s(k):
        return [b for b in range(4) if b not in VC[k]]

    def cast(t, k, b):
        n, z = NB[k], 4 * (C * t + C0[k])
        out, in_ = T.zt[:, z + b:z + 4 * n:4], T.ps[:, 512 * (4 * k + b):512 * (4 * k + b) + n]
        v = b in on_v(k)
        st[t, k, "c", b] = bank[4 * k + b] = run("V" if v else "S", [st[t, k, "z", b]], cp(out, in_) if v else act(out, in_))

    def qz(t, k):
        n, a = NB[k], C * t + C0[k]
        st[t, k, "qz"] = run("V", [st[t, k, "c", b] for b in range(4)], quant(T.zq[:, a:a + n], T.zs[:, a:a + n], T.zt[:, 4 * a:4 * a + 4 * n]))

    def wprod(t, k):
        n, a = NB[k], C * t + C0[k]
        for b in range(4):
            st[t, k, "r", b] = run("T", [("dW", 32), st[t, k, "qz"], bank.get(4 * k + b)],
                                   mm(4 * k + b, n, T.wq[:, 128 * b:128 * b + 128], T.wsc[:, 128 * b:128 * b + 128], T.zq[:, a:a + n], T.zs[:, a:a + n]))

    def xupd(t, k, bs_):
        n, a, e = NB[k], 4 * C0[k], 4 * (C0[k] + NB[k])
        for b in bs_:
            st[t, k, "x", b] = bank[4 * k + b] = run(
                "V", [st[t, k, "r", b], ("dXA", 16) if t == 0 and k == 0 else ("dXB", 16) if t == 0 else st[t - 1, k, "x", b]],
                tt(XT[t + 1][:, a + b:e:4], T.ps[:, 512 * (4 * k + b):512 * (4 * k + b) + n], XT[t][:, a + b:e:4], O.add))

    def newx(t, k):
        quantx(t + 1, k, [st[t, k, "x", b] for b in range(4)])

    def yprod(k):
        n = NB[k]
        bk = 4 * k
        return run("T", [vq, qx[R, k], bank.get(bk)], mm(bk, n, T.vq[:, :], T.vs[:, :], T.q3[:, sl(k)], T.s3[:, sl(k)]))

    pf = run("V", [("dP", 16)], cp(T.pfl[0:1, :], T.pin[0:1, :]))
    pb = run("G", [pf], lambda: g.partition_broadcast(T.pbc[:, :], T.pfl[0:1, :], 128))
    quantx(0, 0, [("dXA", 16)])
    send(0)
    uq = run("V", [("dU", 16)], quant(T.uq[:, :], T.us[:, :], T.ut[:, :]))
    u2 += [run("V", [uq, c_off0], cp(T.u2q[:, 0:128].bitcast(dt.uint32), T.uq[:, 0:128].bitcast(dt.uint32).indirect(T.off0[:, 0:8]))),
           run("S", [uq, c_off0], act(T.u2s[:, 0:128], T.us[:, 0:128].indirect(T.off0[:, 0:8])))]
    sprod(0, 0)
    equant(1, 0)
    equant(1, 1)
    chain1(0, 0, [lambda: equant(1, 2), lambda: equant(1, 3)])
    gath(0, 0)
    count_on(0, 0)
    for lo, hi in ((256, 512), (512, 768), (768, TAB)):
        m_t.append(run("S", m_t[:1], act(T.tab[:, lo:hi], T.tab[:, 0:hi - lo])))
    pm = [run("V", [pb, (a_m0, a_m1)[l]], tt(T.pm[:, 8 * l:8 * l + 8], T.pbc[:, :], T.mk[:, 8 * l:8 * l + 8], O.mult)) for l in range(2)]
    sc = [run("V", [pm[l]], lambda l=l: g.vector.tensor_reduce(col(3 + l), T.pm[:, 8 * l:8 * l + 8], AxisListType.X, O.add)) for l in range(2)]
    quantx(0, 1, [("dXB", 16)])
    cc2, bs = [], [[], []]

    def c_cc():
        for l in range(2):
            cc2.append(run("V", [sc[l], k_q], tt(col(7 + l), col(2), col(3 + l), O.subtract)))

    def c_base(k):
        m = NB[k] // 16
        for l in range(2):
            o = 16 * k + m * l
            bs[k].append(run("V", [cc2[l], i_m], ts(T.base[:, o:o + m], T.m16[:, 0:m], col(7 + l), O.add)))

    chain2a(0, 0, [c_cc])
    chain2b(0, 0, [lambda: c_base(0), lambda: equant(2, 0), lambda: equant(2, 1)])
    own(0, 0)
    vq = None

    for t in range(R):
        sprod(t, 1)
        picks(t, 0)
        far(t, 0, 0)
        if t == 0:
            equant(2, 2)
            equant(2, 3)
        far(t, 0, 1)
        for b in on_s(0):
            cast(t, 0, b)
        chain1(t, 1, [lambda: None] + [lambda b=b: cast(t, 0, b) for b in on_v(0)])
        gath(t, 1)
        count_on(t, 1)
        own(t, 1, (0, 1))
        qz(t, 0)
        wprod(t, 0)
        own(t, 1, (2, 3))
        if t == 0:
            c_base(1)
        xs = [lambda b=b: xupd(t, 0, (b,)) for b in range(4)]
        chain2a(t, 1, xs)
        chain2b(t, 1, xs)
        for f in xs:
            f()
        newx(t, 0)
        if t < R - 1:
            send(t + 1)
            picks(t, 1)
            sprod(t + 1, 0)
            far(t, 1, 0)
            far(t, 1, 1)
            chain1(t + 1, 0)
            gath(t + 1, 0)
            for b in on_s(1) + list(on_v(1)[:-1]):
                cast(t, 1, b)
            count_on(t + 1, 0)

            def zb():
                for b in on_v(1)[-1:]:
                    cast(t, 1, b)
                qz(t, 1)
            chain2a(t + 1, 0, [zb])
            wprod(t, 1)
            xs = [lambda b=b: xupd(t, 1, (b,)) for b in range(4)]
            chain2b(t + 1, 0, [lambda: None] + xs)
            for b in range(2, 4):
                xs[b]()
            newx(t, 1)
            own(t + 1, 0)
        else:
            picks(t, 1)
            far(t, 1, 0)
            far(t, 1, 1)
            vq = run("V", [("dV", 16)], quant(T.vq[:, :], T.vs[:, :], T.vt[:, :]))
            ns = [run("V", [sc[l]], ts(col(5 + l), col(3 + l), -1.0, O.mult)) for l in range(2)]
            y0 = yprod(0)
            for b in range(4):
                cast(t, 1, b)
            ax = []
            for kk in range(2):
                n, d = NB[kk], 2 * (C * t + C0[kk])
                for l in range(2):
                    ax.append(run("S", st[t, kk, "pl"] + [ns[l]], act((T.ao0, T.ao1)[l][:, sl(kk)], T.pl[:, d + l * n:d + l * n + n], F.Identity, bias=col(5 + l))))
            ys = run("S", [y0], act(T.ysb[:, 0:128], T.ps[:, 0:128]))
            need("Y", [qx[R, 0]])
            g.sync.dma_start(T.oc[:, 0:512], T.q3[:, 0:128].bitcast(dt.uint8)).then_inc(T.sem.outA, 16)
            need("Y", ax)
            for l in range(2):
                g.sync.dma_start(T.ao[l:8:2, :], (T.ao0, T.ao1)[l][0:128:32, :]).then_inc(T.sem.outA, 16)
            need("Y", [ys])
            g.sync.dma_start(T.y[:, 0:128], T.ysb[:, 0:128]).then_inc(T.sem.outA, 16)
            qz(t, 1)
            wprod(t, 1)
            xupd(t, 1, range(4))
            newx(t, 1)
    y1 = run("S", [yprod(1)], act(T.ysb[:, 128:288], T.ps[:, 2048:2208]))
    need("Y", [qx[R, 1]])
    for k in range(3):
        g.sync.dma_start(T.osc[4 * k:4 * k + 4, :], T.s3[32 * k:32 * k + 4, 0:C]).then_inc(T.sem.outA, 16)
    g.scalar.dma_start(T.oc[:, 512:1152], T.q3[:, 128:288].bitcast(dt.uint8)).then_inc(T.sem.outB, 16)
    g.scalar.dma_start(T.osc[12:16, :], T.s3[96:100, 0:C]).then_inc(T.sem.outB, 16)
    need("Y", [y1])
    g.sync.dma_start(T.y[:, 128:288], T.ysb[:, 128:288]).then_inc(T.sem.outA, 16)
    for q in ("V", "S", "T", "G"):
        need("Y", [(q, count[q])])
    g.sync.wait_ge(T.sem.outA, 16 * 8)
    g.scalar.wait_ge(T.sem.outB, 16 * 2)
    g.wait_ge(T.sem.sent, 2 * R * len(topo.engines(core, prev)[::2]))
